import numpy as np
import ml_dtypes


def mxq(x, axis, fmt="e4m3"):
    dtype, down = {"e4m3": (ml_dtypes.float8_e4m3fn, 7), "e5m2": (ml_dtypes.float8_e5m2, 14)}[fmt]
    v = np.moveaxis(np.asarray(x, np.float32).astype(ml_dtypes.bfloat16).astype(np.float64), axis, -1)
    blocks = v.reshape(v.shape[:-1] + (-1, 32))
    amax = np.abs(blocks).max(-1, keepdims=True)
    byte = np.maximum(np.where(amax > 0, np.frexp(amax)[1] - 1 + 127, 0) - down, 1)
    scale = np.exp2(byte - 127.0)
    codes = (blocks / scale).astype(np.float32).astype(dtype).astype(np.float64)
    return np.moveaxis((codes * scale).reshape(v.shape), -1, axis)


WIDE = False


def mx_kscale(k):
    if not WIDE:
        return np.ones(k)
    levels = np.array([10, -10, 5, -5, 0])
    if k % 512:
        return np.exp2(np.random.permutation(np.resize(levels, k // 32))).repeat(32)
    a = np.empty((k // 512, 16))
    for p in range(k // 512):
        a[p, :8] = np.random.permutation(np.resize(levels, 8))
        for g in range(8):
            far = levels[np.abs(levels - a[p, g]) >= 10]
            a[p, g + 8] = far[np.random.randint(len(far))]
    return np.exp2(a.ravel()).repeat(32)


def f64(x):
    return np.asarray(x).astype(np.float64)


def striped(idx):
    return np.tile(idx.reshape(-1, 16).T, (8, 1)).astype(np.uint16)


def unstriped(offs):
    return offs[:16].T.reshape(-1).astype(np.int64)


E2M1 = np.array([0.0, 0.5, 1.0, 1.5, 2.0, 3.0, 4.0, 6.0, -0.0, -0.5, -1.0, -1.5, -2.0, -3.0, -4.0, -6.0])


def pack_weight(w, fmt):
    k, n = w.shape
    w = f64(np.asarray(w, np.float32).astype(ml_dtypes.bfloat16)).reshape(k // 32, 32, n)
    amax = np.abs(w).max(1)
    if fmt == "e4m3":
        byte = np.frexp(amax)[1] - 1 + 127 - 7
    else:
        mant, ex = np.frexp(amax / 6.0)
        byte = np.where(mant > 0.5, ex, ex - 1) + 127
    byte = np.clip(np.where(amax > 0, byte, 1), 1, 254)
    scaled = (w * np.exp2(127.0 - byte)[:, None, :]).reshape(k, n).astype(np.float32)
    by_word = np.ascontiguousarray(scaled.reshape(k // 512, 128, 4, n).transpose(0, 1, 3, 2))
    if fmt == "e4m3":
        words = by_word.astype(ml_dtypes.float8_e4m3fn).view(np.uint8)
    else:
        c = by_word.astype(ml_dtypes.float4_e2m1fn).view(np.uint8) & 0xF
        words = (c[..., 0::2] | (c[..., 1::2] << 4)).reshape(k // 512, 128, 2 * n)
    return np.ascontiguousarray(words), np.ascontiguousarray(byte.astype(np.uint8).reshape(k // 512, 16, n))


def unpack_weight(words, scales, fmt):
    g, _, n = scales.shape
    words = np.ascontiguousarray(words).reshape(g, 128, n, -1)
    if fmt == "e4m3":
        vals = words.view(ml_dtypes.float8_e4m3fn).astype(np.float64)
    else:
        nib = np.empty((g, 128, n, 4), np.uint8)
        nib[..., 0::2] = words & 0xF
        nib[..., 1::2] = words >> 4
        vals = E2M1[nib]
    vals = vals * np.repeat(np.exp2(scales.astype(np.float64) - 127.0), 8, axis=1)[..., None]
    return vals.transpose(0, 1, 3, 2).reshape(g * 512, n)


def relu2(v):
    return np.maximum(v, 0.0) ** 2


K, T, E, C, N = 1024, 1024, 8, 128, 256


def by_expert(wq, xq):
    return np.concatenate([wq[e].T @ xq[:, e * C:(e + 1) * C] for e in range(E)], axis=1)


def setup_inputs():
    n = np.random.standard_normal
    s = mx_kscale(K)[:, None]
    w = [pack_weight(m, "e2m1") for m in n((E + 1, K, N)) / np.sqrt(K) / s[None]]
    return {
        "xT": (n((K, T)) * s).astype(np.float32),
        "w_words": np.stack([m[0] for m in w]),
        "w_scales": np.stack([m[1] for m in w]),
        "b": (0.3 * n((N, E + 1))).astype(np.float32),
        "gate": np.tile(np.random.uniform(0.2, 1.0, E * C), (N, 1)).astype(np.float32),
        "offs": striped(np.random.permutation(T)[:E * C]),
    }


def reference(xT, w_words, w_scales, b, gate, offs):
    idx = unstriped(offs)
    w = np.stack([unpack_weight(w_words[e], w_scales[e], "e2m1") for e in range(E + 1)])
    wq = w
    xs = mxq(f64(xT), 0, "e4m3")
    ys = relu2((wq[E].T @ xs) + f64(b)[:, E:])
    xq = mxq(f64(xT)[:, idx], 0, "e4m3")
    y = by_expert(w, xq)
    y = relu2(y + np.repeat(f64(b)[:, :E], C, axis=1))
    out = ys
    out[:, idx] += f64(gate) * y
    return out

@@ -1,0 +1,167 @@
+from contextlib import ExitStack
+
+import concourse.mybir as mybir
+
+K, T, E, C, N = 1024, 1024, 8, 128, 256
+FLOPS = 2 * 2 * K * T * N
+
+F32 = mybir.dt.float32
+BF16 = mybir.dt.bfloat16
+U32 = mybir.dt.uint32
+I32 = mybir.dt.int32
+U16 = mybir.dt.uint16
+U8 = mybir.dt.uint8
+FP8X4 = mybir.dt.float8_e4m3fn_x4
+FP4X4 = mybir.dt.float4_e2m1fn_x4
+
+ADD = mybir.AluOpType.add
+MULT = mybir.AluOpType.mult
+RELU = mybir.ActivationFunctionType.Relu
+SQUARE = mybir.ActivationFunctionType.Square
+
+P = 128
+A = K // 512
+Q = 256
+NQ = T // Q
+
+
+def tile_moe_shr_lin_relu2_kernel(tc, xT, w_words, w_scales, b, gate, offs, out):
+    nc = tc.nc
+    with ExitStack() as ctx:
+        held = ctx.enter_context(tc.tile_pool(name="held", bufs=1))
+        work = ctx.enter_context(tc.tile_pool(name="work", bufs=3))
+        psum = ctx.enter_context(tc.psum_pool(name="psum", bufs=1))
+
+        offsets = held.tile([P, T // 16], U16, name="offsets")
+        nc.sync.dma_start(offsets[:], offs)
+
+        dummy = held.tile([P, 1], F32, name="dummy")
+        nc.vector.memset(dummy[:], 0.0)
+        nc.scalar.activation(dummy[:], dummy[:], RELU)
+
+        planes = held.tile([P, (E + 1) * A, N], U8, name="planes", align_bytes=64)
+        nc.gpsimd.memset(planes[:].bitcast(I32), 0)
+
+        x_view = xT.rearrange("(a p u e) n -> a u p e n", p=P, u=2, e=2)
+        raws = {}
+
+        def load_x(a, u):
+            for s in range(2):
+                raw = held.tile([P, 2, 512], F32, name=f"raw{a}{u}{s}")
+                nc.sync.dma_start(raw[:], x_view[a, u][:, :, 512 * s : 512 * s + 512])
+                raws[a, u, s] = raw
+
+        w_view = w_words.bitcast(I32)
+        w_at = {}
+
+        def load_w(first, count):
+            tile = held.tile([P, count * A, 2 * N], U8, name=f"words{first}", align_bytes=64)
+            nc.sync.dma_start(tile[:].bitcast(I32), w_view[first : first + count].rearrange("e a p c -> p (e a) c"))
+            for i in range(count):
+                w_at[first + i] = (tile, i * A)
+
+        s_view = w_scales.bitcast(I32)
+        load_x(0, 0)
+        load_x(0, 1)
+        load_x(1, 0)
+        for quad in range(4):
+            nc.sync.dma_start(
+                planes[32 * quad : 32 * quad + 4].bitcast(I32),
+                s_view[:, :, 4 * quad : 4 * quad + 4, :].rearrange("e a q n -> q (e a) n"),
+            )
+        load_x(1, 1)
+        load_w(8, 1)
+        load_w(0, 2)
+        bias = held.tile([P, 2, E + 1], F32, name="bias")
+        nc.sync.dma_start(bias[:], b.rearrange("(h p) e -> p h e", p=P))
+        load_w(2, 3)
+        gates = held.tile([P, T], F32, name="gates")
+        nc.sync.dma_start(gates[:], gate[0:P, :])
+        load_w(5, 3)
+
+        pairs = {}
+        grouped = {}
+        for a in range(A):
+            for q in range(NQ):
+                grouped[a, q] = None
+
+        def cast(a, u):
+            pair = held.tile([P, T, 2], BF16, name=f"pair{a}{u}", align_bytes=64)
+            pairs[a, u] = pair
+            for s in range(2):
+                dst = pair[:, 512 * s : 512 * s + 512, :]
+                src = raws[a, u, s][:].rearrange("p e n -> p n e")
+                if (a, u, s) == (0, 0, 1):
+                    nc.vector.tensor_copy(dst, src)
+                else:
+                    nc.scalar.copy(dst, src)
+
+        def gather(a, u, dst, first, count):
+            window = pairs[a, u][:].rearrange("p n e -> p (n e)").bitcast(U32)
+            idx = offsets[:, first // 16 : (first + count) // 16]
+            nc.vector.tensor_copy(dst.bitcast(U32)[:, :, u], window.indirect(idx))
+
+        codes = [held.tile([P, T], U32, name=f"codes{a}", align_bytes=64) for a in range(A)]
+        scales = [held.tile([P, T], U8, name=f"scales{a}", align_bytes=64) for a in range(A)]
+
+        def quantize(a, g, first, count):
+            nc.vector.quantize_mx(
+                out=codes[a][:, first : first + count].bitcast(FP8X4),
+                scales=scales[a][:, first : first + count],
+                in_=g.rearrange("p n j -> p (n j)"),
+            )
+
+        g0 = [held.tile([P, 512, 4], BF16, name=f"g0_{i}", align_bytes=64) for i in range(2)]
+        g1 = [held.tile([P, Q, 4], BF16, name=f"g1_{i}", align_bytes=64) for i in range(NQ)]
+
+        cast(0, 0)
+        for i in range(2):
+            gather(0, 0, g0[i][:], 512 * i, 512)
+        cast(0, 1)
+        for i in range(2):
+            gather(0, 1, g0[i][:], 512 * i, 512)
+        cast(1, 0)
+        quantize(0, g0[0][:], 0, 512)
+        quantize(0, g0[1][:], 512, 512)
+        for i in range(NQ):
+            gather(1, 0, g1[i][:], Q * i, Q)
+        cast(1, 1)
+        gather(1, 1, g1[0][:], 0, Q)
+        for i in range(NQ):
+            if i + 1 < NQ:
+                gather(1, 1, g1[i + 1][:], Q * (i + 1), Q)
+            quantize(1, g1[i][:], Q * i, Q)
+
+        for h in range(2):
+            window = held.tile([P, T], F32, name=f"window{h}")
+            for q in range(NQ):
+                bank = psum.tile([P, 4, C], F32, name=f"bank{h}{q}")
+                for j in range(4):
+                    e = 2 * q + j if j < 2 else E
+                    slots = slice(Q * q + C * (j % 2), Q * q + C * (j % 2) + C)
+                    tile, at = w_at[e]
+                    for a in range(A):
+                        nc.tensor.matmul_mx(
+                            out=bank[:, j, :],
+                            lhsT=tile[:, at + a, N * h : N * h + N].bitcast(FP4X4),
+                            lhsT_scale=planes[:, e * A + a, P * h : P * h + P],
+                            rhs=codes[a][:, slots].bitcast(FP8X4),
+                            rhs_scale=scales[a][:, slots],
+                            start=(a == 0),
+                            stop=(a == A - 1),
+                        )
+                r = work.tile([P, 4, C], F32, name="r")
+                for j in range(2):
+                    e = 2 * q + j
+                    nc.scalar.activation(r[:, j, :], bank[:, j, :], RELU, bias=bias[:, h, e : e + 1])
+                nc.scalar.activation(r[:, 2:4, :], bank[:, 2:4, :], RELU, bias=bias[:, h, E : E + 1])
+                sq = work.tile([P, 4, C], F32, name="sq")
+                nc.scalar.activation(sq[:], r[:], SQUARE)
+                t = work.tile([P, Q], F32, name="t")
+                o = work.tile([P, Q], F32, name="o")
+                flat = sq[:].rearrange("p j c -> p (j c)")
+                eng = nc.vector if (h, q) == (0, 0) else nc.gpsimd
+                eng.tensor_tensor(t[:], flat[:, 0:Q], gates[:, Q * q : Q * q + Q], MULT)
+                eng.tensor_tensor(o[:], t[:], flat[:, Q : 2 * Q], ADD)
+                nc.vector.tensor_copy(window[:].indirect(offsets[:, Q * q // 16 : Q * (q + 1) // 16]), o[:])
+            nc.sync.dma_start(out[P * h : P * h + P, :], window[:])

@@ -33,7 +33,6 @@ def tile_moe_shr_lin_relu2_kernel(tc, xT, w_words, w_scales, b, gate, offs, out)
         psum = ctx.enter_context(tc.psum_pool(name="psum", bufs=1))
 
         offsets = held.tile([P, T // 16], U16, name="offsets")
-        nc.sync.dma_start(offsets[:], offs)
 
         dummy = held.tile([P, 1], F32, name="dummy")
         nc.vector.memset(dummy[:], 0.0)
@@ -47,7 +46,7 @@ def tile_moe_shr_lin_relu2_kernel(tc, xT, w_words, w_scales, b, gate, offs, out)
 
         def load_x(a, u):
             for s in range(2):
-                raw = held.tile([P, 2, 512], F32, name=f"raw{a}{u}{s}")
+                raw = held.tile([P, 2, 512], F32, name=f"raw{a}{u}{s}", align_bytes=64)
                 nc.sync.dma_start(raw[:], x_view[a, u][:, :, 512 * s : 512 * s + 512])
                 raws[a, u, s] = raw
 
@@ -62,6 +61,7 @@ def tile_moe_shr_lin_relu2_kernel(tc, xT, w_words, w_scales, b, gate, offs, out)
 
         s_view = w_scales.bitcast(I32)
         load_x(0, 0)
+        nc.sync.dma_start(offsets[:], offs)
         load_x(0, 1)
         load_x(1, 0)
         for quad in range(4):
@@ -74,94 +74,125 @@ def tile_moe_shr_lin_relu2_kernel(tc, xT, w_words, w_scales, b, gate, offs, out)
         load_w(0, 2)
         bias = held.tile([P, 2, E + 1], F32, name="bias")
         nc.sync.dma_start(bias[:], b.rearrange("(h p) e -> p h e", p=P))
-        load_w(2, 3)
         gates = held.tile([P, T], F32, name="gates")
-        nc.sync.dma_start(gates[:], gate[0:P, :])
-        load_w(5, 3)
+        nc.sync.dma_start(gates[:, 0:512], gate[0:P, 0:512])
+        load_w(2, 2)
+        load_w(4, 4)
+        nc.sync.dma_start(gates[:, 512:T], gate[0:P, 512:T])
 
+        copies = {"S": nc.scalar.copy, "V": nc.vector.tensor_copy, "G": nc.gpsimd.tensor_copy}
         pairs = {}
-        grouped = {}
-        for a in range(A):
-            for q in range(NQ):
-                grouped[a, q] = None
 
-        def cast(a, u):
+        def cast(a, u, parts):
             pair = held.tile([P, T, 2], BF16, name=f"pair{a}{u}", align_bytes=64)
             pairs[a, u] = pair
-            for s in range(2):
-                dst = pair[:, 512 * s : 512 * s + 512, :]
-                src = raws[a, u, s][:].rearrange("p e n -> p n e")
-                if (a, u, s) == (0, 0, 1):
-                    nc.vector.tensor_copy(dst, src)
-                else:
-                    nc.scalar.copy(dst, src)
+            for engine, first, last in parts:
+                at = first % 512
+                copies[engine](pair[:, first:last, :], raws[a, u, first // 512][:, :, at : at + last - first].rearrange("p e n -> p n e"))
 
         def gather(a, u, dst, first, count):
             window = pairs[a, u][:].rearrange("p n e -> p (n e)").bitcast(U32)
             idx = offsets[:, first // 16 : (first + count) // 16]
-            nc.vector.tensor_copy(dst.bitcast(U32)[:, :, u], window.indirect(idx))
+            nc.vector.tensor_copy(dst.rearrange("p (n u) -> p n u", u=2)[:, :, u], window.indirect(idx))
 
-        codes = [held.tile([P, T], U32, name=f"codes{a}", align_bytes=64) for a in range(A)]
-        scales = [held.tile([P, T], U8, name=f"scales{a}", align_bytes=64) for a in range(A)]
+        codes = {}
+        scales = {}
 
-        def quantize(a, g, first, count):
+        def quantize(a, i, words, first, count):
             nc.vector.quantize_mx(
-                out=codes[a][:, first : first + count].bitcast(FP8X4),
-                scales=scales[a][:, first : first + count],
-                in_=g.rearrange("p n j -> p (n j)"),
+                out=codes[a, i][:, first : first + count].bitcast(FP8X4),
+                scales=scales[a, i][:, first : first + count],
+                in_=words[:, 2 * first : 2 * (first + count)].bitcast(BF16),
             )
 
-        g0 = [held.tile([P, 512, 4], BF16, name=f"g0_{i}", align_bytes=64) for i in range(2)]
-        g1 = [held.tile([P, Q, 4], BF16, name=f"g1_{i}", align_bytes=64) for i in range(NQ)]
+        for a in range(A):
+            for i in range(2):
+                scales[a, i] = held.tile([P, 512], U8, name=f"scales{a}{i}", align_bytes=64)
+                if (a, i) != (0, 1):
+                    codes[a, i] = held.tile([P, 512], U32, name=f"codes{a}{i}", align_bytes=64)[:]
+        words0 = [held.tile([P, 1024], U32, name=f"words0_{i}", align_bytes=64) for i in range(2)]
 
-        cast(0, 0)
+        cast(0, 0, [("S", 0, 512), ("V", 512, 896), ("S", 896, 1024)])
         for i in range(2):
-            gather(0, 0, g0[i][:], 512 * i, 512)
-        cast(0, 1)
+            gather(0, 0, words0[i][:], 512 * i, 512)
+        cast(0, 1, [("S", 0, 512), ("S", 512, 768), ("G", 768, 1024)])
         for i in range(2):
-            gather(0, 1, g0[i][:], 512 * i, 512)
-        cast(1, 0)
-        quantize(0, g0[0][:], 0, 512)
-        quantize(0, g0[1][:], 512, 512)
-        for i in range(NQ):
-            gather(1, 0, g1[i][:], Q * i, Q)
-        cast(1, 1)
-        gather(1, 1, g1[0][:], 0, Q)
-        for i in range(NQ):
-            if i + 1 < NQ:
-                gather(1, 1, g1[i + 1][:], Q * (i + 1), Q)
-            quantize(1, g1[i][:], Q * i, Q)
+            gather(0, 1, words0[i][:], 512 * i, 512)
+        cast(1, 0, [("S", 0, 512), ("S", 512, 1024)])
+        early = held.tile([P, 1024], U32, name="turns", align_bytes=64)
+        gather(1, 0, early[:], 0, 512)
+        quantize(0, 0, words0[0][:], 0, 512)
+        cast(1, 1, [("S", 0, 512), ("S", 512, 1024)])
+        for q in range(2):
+            gather(1, 1, early[:, 512 * q : 512 * q + 512], Q * q, Q)
+        for q in range(2):
+            quantize(1, 0, early[:], Q * q, Q)
+        late = held.tile([P, 1024], U32, name="turns", align_bytes=64)
+        codes[0, 1] = held.tile([P, 512], U32, name="raw111", align_bytes=64)[:]
+        gather(1, 0, late[:], 512, 512)
+        gather(1, 1, late[:], 512, 512)
+        quantize(0, 1, words0[1][:], 0, 512)
+        quantize(1, 1, late[:], 0, 512)
 
+        windows = [held.tile([P, T], F32, name=f"window{h}") for h in range(2)]
+
+        def product(out_ap, e, h, i, first, count):
+            tile, at = w_at[e]
+            for a in range(A):
+                nc.tensor.matmul_mx(
+                    out=out_ap,
+                    lhsT=tile[:, at + a, N * h : N * h + N].bitcast(FP4X4),
+                    lhsT_scale=planes[:, e * A + a, P * h : P * h + P],
+                    rhs=codes[a, i][:, first : first + count].bitcast(FP8X4),
+                    rhs_scale=scales[a, i][:, first : first + count],
+                    start=(a == 0),
+                    stop=(a == A - 1),
+                )
+
+        def combine(h, first, sq_y, sq_s, engines):
+            t = work.tile([P, Q], F32, name="t")
+            o = work.tile([P, Q], F32, name="o")
+            engines[0].tensor_tensor(t[:], sq_y, gates[:, first : first + Q], MULT)
+            engines[1].tensor_tensor(o[:], t[:], sq_s, ADD)
+            nc.vector.tensor_copy(windows[h][:].indirect(offsets[:, first // 16 : (first + Q) // 16]), o[:])
+
+        def small_unit(h, q, engines):
+            bank = psum.tile([P, 4, C], F32, name=f"bank{h}{q}")
+            for j in range(2):
+                product(bank[:, j, :], 2 * q + j, h, 0, Q * q + C * j, C)
+            for j in range(2):
+                product(bank[:, 2 + j, :], E, h, 0, Q * q + C * j, C)
+            r = work.tile([P, 4, C], F32, name="r")
+            for j in range(2):
+                e = 2 * q + j
+                nc.scalar.activation(r[:, j, :], bank[:, j, :], RELU, bias=bias[:, h, e : e + 1])
+            nc.scalar.activation(r[:, 2:4, :], bank[:, 2:4, :], RELU, bias=bias[:, h, E : E + 1])
+            sq = work.tile([P, 4 * C], F32, name="sq")
+            nc.scalar.activation(sq[:], r[:].rearrange("p j c -> p (j c)"), SQUARE)
+            combine(h, Q * q, sq[:, 0:Q], sq[:, Q : 2 * Q], engines)
+
+        def big_unit(h, engines):
+            y = psum.tile([P, 4, C], F32, name=f"bank_y{h}")
+            s = psum.tile([P, 4 * C], F32, name=f"bank_s{h}")
+            for j in range(4):
+                product(y[:, j, :], 4 + j, h, 1, C * j, C)
+            product(s[:], E, h, 1, 0, 512)
+            r = work.tile([P, 8, C], F32, name="r_big")
+            sq = work.tile([P, 8 * C], F32, name="sq_big")
+            for j in range(4):
+                e = 4 + j
+                nc.scalar.activation(r[:, j, :], y[:, j, :], RELU, bias=bias[:, h, e : e + 1])
+            nc.scalar.activation(sq[:, 0:512], r[:, 0:4, :].rearrange("p j c -> p (j c)"), SQUARE)
+            nc.scalar.activation(r[:, 4:8, :].rearrange("p j c -> p (j c)"), s[:], RELU, bias=bias[:, h, E : E + 1])
+            nc.scalar.activation(sq[:, 512:1024], r[:, 4:8, :].rearrange("p j c -> p (j c)"), SQUARE)
+            for i in range(2):
+                combine(h, 512 + Q * i, sq[:, Q * i : Q * i + Q], sq[:, 512 + Q * i : 512 + Q * i + Q], engines[i])
+
+        V, G = nc.vector, nc.gpsimd
+        small_unit(0, 0, (V, V))
+        small_unit(1, 0, (G, G))
+        small_unit(0, 1, (G, G))
+        small_unit(1, 1, (G, G))
         for h in range(2):
-            window = held.tile([P, T], F32, name=f"window{h}")
-            for q in range(NQ):
-                bank = psum.tile([P, 4, C], F32, name=f"bank{h}{q}")
-                for j in range(4):
-                    e = 2 * q + j if j < 2 else E
-                    slots = slice(Q * q + C * (j % 2), Q * q + C * (j % 2) + C)
-                    tile, at = w_at[e]
-                    for a in range(A):
-                        nc.tensor.matmul_mx(
-                            out=bank[:, j, :],
-                            lhsT=tile[:, at + a, N * h : N * h + N].bitcast(FP4X4),
-                            lhsT_scale=planes[:, e * A + a, P * h : P * h + P],
-                            rhs=codes[a][:, slots].bitcast(FP8X4),
-                            rhs_scale=scales[a][:, slots],
-                            start=(a == 0),
-                            stop=(a == A - 1),
-                        )
-                r = work.tile([P, 4, C], F32, name="r")
-                for j in range(2):
-                    e = 2 * q + j
-                    nc.scalar.activation(r[:, j, :], bank[:, j, :], RELU, bias=bias[:, h, e : e + 1])
-                nc.scalar.activation(r[:, 2:4, :], bank[:, 2:4, :], RELU, bias=bias[:, h, E : E + 1])
-                sq = work.tile([P, 4, C], F32, name="sq")
-                nc.scalar.activation(sq[:], r[:], SQUARE)
-                t = work.tile([P, Q], F32, name="t")
-                o = work.tile([P, Q], F32, name="o")
-                flat = sq[:].rearrange("p j c -> p (j c)")
-                eng = nc.vector if (h, q) == (0, 0) else nc.gpsimd
-                eng.tensor_tensor(t[:], flat[:, 0:Q], gates[:, Q * q : Q * q + Q], MULT)
-                eng.tensor_tensor(o[:], t[:], flat[:, Q : 2 * Q], ADD)
-                nc.vector.tensor_copy(window[:].indirect(offsets[:, Q * q // 16 : Q * (q + 1) // 16]), o[:])
-            nc.sync.dma_start(out[P * h : P * h + P, :], window[:])
+            big_unit(h, [(G, G), (G, G)])
+            nc.sync.dma_start(out[P * h : P * h + P, :], windows[h][:])

from contextlib import ExitStack

import concourse.mybir as mybir

K, T, E, C, N = 1024, 1024, 8, 128, 256
FLOPS = 2 * 2 * K * T * N

F32 = mybir.dt.float32
BF16 = mybir.dt.bfloat16
U32 = mybir.dt.uint32
I32 = mybir.dt.int32
U16 = mybir.dt.uint16
U8 = mybir.dt.uint8
FP8X4 = mybir.dt.float8_e4m3fn_x4
FP4X4 = mybir.dt.float4_e2m1fn_x4

ADD = mybir.AluOpType.add
MULT = mybir.AluOpType.mult
RELU = mybir.ActivationFunctionType.Relu
SQUARE = mybir.ActivationFunctionType.Square

P = 128
A = K // 512
Q = 256
NQ = T // Q


def tile_moe_shr_lin_relu2_kernel(tc, xT, w_words, w_scales, b, gate, offs, out):
    nc = tc.nc
    with ExitStack() as ctx:
        held = ctx.enter_context(tc.tile_pool(name="held", bufs=1))
        work = ctx.enter_context(tc.tile_pool(name="work", bufs=3))
        psum = ctx.enter_context(tc.psum_pool(name="psum", bufs=1))

        offsets = held.tile([P, T // 16], U16, name="offsets")

        dummy = held.tile([P, 1], F32, name="dummy")
        nc.vector.memset(dummy[:], 0.0)
        nc.scalar.activation(dummy[:], dummy[:], RELU)

        planes = held.tile([P, (E + 1) * A, N], U8, name="planes", align_bytes=64)
        nc.gpsimd.memset(planes[:].bitcast(I32), 0)

        x_view = xT.rearrange("(a p u e) n -> a u p e n", p=P, u=2, e=2)
        raws = {}

        def load_x(a, u):
            for s in range(2):
                raw = held.tile([P, 2, 512], F32, name=f"raw{a}{u}{s}", align_bytes=64)
                nc.sync.dma_start(raw[:], x_view[a, u][:, :, 512 * s : 512 * s + 512])
                raws[a, u, s] = raw

        w_view = w_words.bitcast(I32)
        w_at = {}

        def load_w(first, count):
            tile = held.tile([P, count * A, 2 * N], U8, name=f"words{first}", align_bytes=64)
            nc.sync.dma_start(tile[:].bitcast(I32), w_view[first : first + count].rearrange("e a p c -> p (e a) c"))
            for i in range(count):
                w_at[first + i] = (tile, i * A)

        s_view = w_scales.bitcast(I32)
        load_x(0, 0)
        nc.sync.dma_start(offsets[:], offs)
        load_x(0, 1)
        load_x(1, 0)
        for quad in range(4):
            nc.sync.dma_start(
                planes[32 * quad : 32 * quad + 4].bitcast(I32),
                s_view[:, :, 4 * quad : 4 * quad + 4, :].rearrange("e a q n -> q (e a) n"),
            )
        load_x(1, 1)
        load_w(8, 1)
        load_w(0, 2)
        bias = held.tile([P, 2, E + 1], F32, name="bias")
        nc.sync.dma_start(bias[:], b.rearrange("(h p) e -> p h e", p=P))
        gates = held.tile([P, T], F32, name="gates")
        nc.sync.dma_start(gates[:, 0:512], gate[0:P, 0:512])
        load_w(2, 2)
        load_w(4, 4)
        nc.sync.dma_start(gates[:, 512:T], gate[0:P, 512:T])

        copies = {"S": nc.scalar.copy, "V": nc.vector.tensor_copy, "G": nc.gpsimd.tensor_copy}
        pairs = {}

        def cast(a, u, parts):
            pair = held.tile([P, T, 2], BF16, name=f"pair{a}{u}", align_bytes=64)
            pairs[a, u] = pair
            for engine, first, last in parts:
                at = first % 512
                copies[engine](pair[:, first:last, :], raws[a, u, first // 512][:, :, at : at + last - first].rearrange("p e n -> p n e"))

        def gather(a, u, dst, first, count):
            window = pairs[a, u][:].rearrange("p n e -> p (n e)").bitcast(U32)
            idx = offsets[:, first // 16 : (first + count) // 16]
            nc.vector.tensor_copy(dst.rearrange("p (n u) -> p n u", u=2)[:, :, u], window.indirect(idx))

        codes = {}
        scales = {}

        def quantize(a, i, words, first, count):
            nc.vector.quantize_mx(
                out=codes[a, i][:, first : first + count].bitcast(FP8X4),
                scales=scales[a, i][:, first : first + count],
                in_=words[:, 2 * first : 2 * (first + count)].bitcast(BF16),
            )

        for a in range(A):
            for i in range(2):
                scales[a, i] = held.tile([P, 512], U8, name=f"scales{a}{i}", align_bytes=64)
                if (a, i) != (0, 1):
                    codes[a, i] = held.tile([P, 512], U32, name=f"codes{a}{i}", align_bytes=64)[:]
        words0 = [held.tile([P, 1024], U32, name=f"words0_{i}", align_bytes=64) for i in range(2)]

        cast(0, 0, [("S", 0, 512), ("V", 512, 896), ("S", 896, 1024)])
        for i in range(2):
            gather(0, 0, words0[i][:], 512 * i, 512)
        cast(0, 1, [("S", 0, 512), ("S", 512, 768), ("G", 768, 1024)])
        for i in range(2):
            gather(0, 1, words0[i][:], 512 * i, 512)
        cast(1, 0, [("S", 0, 512), ("S", 512, 1024)])
        early = held.tile([P, 1024], U32, name="turns", align_bytes=64)
        gather(1, 0, early[:], 0, 512)
        quantize(0, 0, words0[0][:], 0, 512)
        cast(1, 1, [("S", 0, 512), ("S", 512, 1024)])
        for q in range(2):
            gather(1, 1, early[:, 512 * q : 512 * q + 512], Q * q, Q)
        for q in range(2):
            quantize(1, 0, early[:], Q * q, Q)
        late = held.tile([P, 1024], U32, name="turns", align_bytes=64)
        codes[0, 1] = held.tile([P, 512], U32, name="raw111", align_bytes=64)[:]
        gather(1, 0, late[:], 512, 512)
        gather(1, 1, late[:], 512, 512)
        quantize(0, 1, words0[1][:], 0, 512)
        quantize(1, 1, late[:], 0, 512)

        windows = [held.tile([P, T], F32, name=f"window{h}") for h in range(2)]

        def product(out_ap, e, h, i, first, count):
            tile, at = w_at[e]
            for a in range(A):
                nc.tensor.matmul_mx(
                    out=out_ap,
                    lhsT=tile[:, at + a, N * h : N * h + N].bitcast(FP4X4),
                    lhsT_scale=planes[:, e * A + a, P * h : P * h + P],
                    rhs=codes[a, i][:, first : first + count].bitcast(FP8X4),
                    rhs_scale=scales[a, i][:, first : first + count],
                    start=(a == 0),
                    stop=(a == A - 1),
                )

        def combine(h, first, sq_y, sq_s, engines):
            t = work.tile([P, Q], F32, name="t")
            o = work.tile([P, Q], F32, name="o")
            engines[0].tensor_tensor(t[:], sq_y, gates[:, first : first + Q], MULT)
            engines[1].tensor_tensor(o[:], t[:], sq_s, ADD)
            nc.vector.tensor_copy(windows[h][:].indirect(offsets[:, first // 16 : (first + Q) // 16]), o[:])

        def small_unit(h, q, engines):
            bank = psum.tile([P, 4, C], F32, name=f"bank{h}{q}")
            for j in range(2):
                product(bank[:, j, :], 2 * q + j, h, 0, Q * q + C * j, C)
            for j in range(2):
                product(bank[:, 2 + j, :], E, h, 0, Q * q + C * j, C)
            r = work.tile([P, 4, C], F32, name="r")
            for j in range(2):
                e = 2 * q + j
                nc.scalar.activation(r[:, j, :], bank[:, j, :], RELU, bias=bias[:, h, e : e + 1])
            nc.scalar.activation(r[:, 2:4, :], bank[:, 2:4, :], RELU, bias=bias[:, h, E : E + 1])
            sq = work.tile([P, 4 * C], F32, name="sq")
            nc.scalar.activation(sq[:], r[:].rearrange("p j c -> p (j c)"), SQUARE)
            combine(h, Q * q, sq[:, 0:Q], sq[:, Q : 2 * Q], engines)

        def big_unit(h, engines):
            y = psum.tile([P, 4, C], F32, name=f"bank_y{h}")
            s = psum.tile([P, 4 * C], F32, name=f"bank_s{h}")
            for j in range(4):
                product(y[:, j, :], 4 + j, h, 1, C * j, C)
            product(s[:], E, h, 1, 0, 512)
            r = work.tile([P, 8, C], F32, name="r_big")
            sq = work.tile([P, 8 * C], F32, name="sq_big")
            for j in range(4):
                e = 4 + j
                nc.scalar.activation(r[:, j, :], y[:, j, :], RELU, bias=bias[:, h, e : e + 1])
            nc.scalar.activation(sq[:, 0:512], r[:, 0:4, :].rearrange("p j c -> p (j c)"), SQUARE)
            nc.scalar.activation(r[:, 4:8, :].rearrange("p j c -> p (j c)"), s[:], RELU, bias=bias[:, h, E : E + 1])
            nc.scalar.activation(sq[:, 512:1024], r[:, 4:8, :].rearrange("p j c -> p (j c)"), SQUARE)
            for i in range(2):
                combine(h, 512 + Q * i, sq[:, Q * i : Q * i + Q], sq[:, 512 + Q * i : 512 + Q * i + Q], engines[i])

        V, G = nc.vector, nc.gpsimd
        small_unit(0, 0, (V, V))
        small_unit(1, 0, (G, G))
        small_unit(0, 1, (G, G))
        small_unit(1, 1, (G, G))
        for h in range(2):
            big_unit(h, [(G, G), (G, G)])
            nc.sync.dma_start(out[P * h : P * h + P, :], windows[h][:])
